import numpy as np, ml_dtypes
CORES = [4,20,60,84,92,100,116]
N = 7
F = 256
def setup_inputs(rng):
    return {"a": rng.standard_normal((N, 128, 128), dtype=np.float32).astype(ml_dtypes.bfloat16), "w": rng.standard_normal((N, 128, F), dtype=np.float32).astype(ml_dtypes.bfloat16)}
def setup_inputs_big(rng):
    d = setup_inputs(rng)
    for k in ("a", "w"): d[k] = (d[k].astype(np.float32) * 1024.0).astype(d[k].dtype)
    return d
def setup_inputs_small(rng):
    d = setup_inputs(rng)
    for k in ("a", "w"): d[k] = (d[k].astype(np.float32) * (1 / 1024.0)).astype(d[k].dtype)
    return d
def setup_inputs_apart(rng):
    d = setup_inputs(rng)
    f = (10.0 ** rng.permutation(np.linspace(-1.5, 1.5, N))).astype(np.float32).reshape(N, 1, 1)
    for k in ("a", "w"): d[k] = (d[k].astype(np.float32) * f).astype(d[k].dtype)
    return d
def reference(a, w):
    A, W = a.astype(np.float64), w.astype(np.float64)
    p = np.stack([A[j].T @ W[j] for j in range(N)])
    return {"y": np.cumsum(p, axis=0).astype(ml_dtypes.bfloat16 if a.dtype != np.float64 else np.float64)}

@@ -1,0 +1,138 @@
+from concourse.bass import DstId, RemoteDMATransfer
+from concourse.mybir import AluOpType
+
+F = 256
+NLAND = 5
+SCRATCH = {
+    "a_sb": ("sbuf", [128, 128], "bfloat16"),
+    "w_sb": ("sbuf", [128, F], "bfloat16"),
+    "ps": ("psum", [128, F], "float32"),
+    "p": ("sbuf", [128, F], "bfloat16"),
+    "ysb": ("sbuf", [128, F], "bfloat16"),
+}
+for _k in range(NLAND):
+    SCRATCH["land%d" % _k] = ("sbuf", [128, F], "bfloat16")
+SEMAPHORES = ["ld", "mm", "cp", "acc", "st", "sent"] + ["arr%d" % _k for _k in range(NLAND)]
+
+NENG = 8
+
+PLAN = [
+    ("r0", (0,), "h3"), ("r0", (0,), "h1"), ("r0", (0,), "r3"), ("r0", (0,), "r6"), ("r0", (0,), "r1"),
+    ("r1", (1,), "h3"), ("r1", (1,), "h1"), ("r1", (1,), "r3"), ("r1", (1,), "r6"),
+    ("r2", (2,), "h4"), ("r2", (2,), "h2"), ("r2", (2,), "r4"),
+    ("r3", (3,), "h3"), ("r3", (3,), "r6"),
+    ("r4", (4,), "h4"),
+    ("r5", (5,), "r6"),
+    ("h1", (0, 1), "r2"),
+    ("h2", (2,), "r3"),
+    ("h3", (0, 1, 3), "r4"), ("h3", (0, 1, 3), "r5"),
+    ("h4", (2, 4), "r5"), ("h4", (2, 4), "r6"),
+]
+
+
+def _bits(mask, n):
+    out, got, e = 0, 0, 0
+    while got < n:
+        if (mask >> e) & 1:
+            out |= 1 << e
+            got += 1
+        e += 1
+    return out
+
+
+def _build(T, topo):
+    cores = list(T.cores)
+    total = topo.CORES_PER_CHIP * topo.CHIPS
+
+    def node(name):
+        c = cores[int(name[1:])]
+        if name[0] == "r":
+            return c
+        return [h for h in range(total)
+                if h not in cores and topo.chip(h) == topo.chip(c) and topo.die(h) == topo.die(c)
+                and all(topo.may_write(h, d) for d in cores)][0]
+
+    msgs = []
+    used = {}
+    pos = {}
+    for s, terms, d in PLAN:
+        src, dst = node(s), node(d)
+        assert topo.may_write(src, dst)
+        slot = used.get(dst, 0)
+        used[dst] = slot + 1
+        pos[src] = pos.get(src, 0) + 1
+        msgs.append({"src": src, "dst": dst, "terms": terms, "slot": slot,
+                     "when": (0 if s[0] == "r" else 1, pos[src])})
+    for m in msgs:
+        common = -1
+        for o in msgs:
+            if o["src"] == m["src"]:
+                common &= topo.mask(o["src"], o["dst"])
+        m["mask"] = _bits(common, NENG)
+        m["n"] = NENG
+    return msgs
+
+
+def rank_program(g, core, T, topo):
+    msgs = _build(T, topo)
+    rank = T.rank_of(core)
+    mine = [m for m in msgs if m["src"] == core]
+    lands = sorted([m for m in msgs if m["dst"] == core], key=lambda m: m["when"])
+    if rank is None and not mine:
+        return
+    S = T.sem
+
+    if rank is not None:
+        got = sorted([rank] + [j for m in lands for j in m["terms"]])
+        assert got == list(range(rank + 1))
+        g.sync.dma_start(T.a_sb[:], T.a[:]).then_inc(S.ld, 16)
+        g.scalar.dma_start(T.w_sb[:], T.w[:]).then_inc(S.ld, 16)
+        g.tensor.wait_ge(S.ld, 32)
+        g.tensor.matmul(T.ps[:], T.a_sb[:], T.w_sb[:], True, True).then_inc(S.mm, 1)
+        g.vector.wait_ge(S.mm, 1)
+        if mine or not lands:
+            g.vector.tensor_copy(T.p[:], T.ps[:]).then_inc(S.cp, 1)
+            g.wait_ge(S.cp, 1)
+
+    waited = set()
+    sent = 0
+    for m in mine:
+        srcs = []
+        for j in m["terms"]:
+            if j == rank:
+                srcs.append(T.p[:])
+                continue
+            l = [x for x in lands if x["terms"] == (j,)][0]
+            if l["slot"] not in waited:
+                g.wait_ge(S["arr%d" % l["slot"]], l["n"])
+                waited.add(l["slot"])
+            srcs.append(T["land%d" % l["slot"]][:])
+        rid, pid, _se = topo.addr(m["dst"])
+        dst_ap = T["land%d" % m["slot"]][:]
+        rsem = S["arr%d" % m["slot"]]
+        if len(srcs) == 1:
+            g.remote_dma(dst_ap, srcs[0], rsem, S.sent, pid, rid, m["mask"])
+        else:
+            g.remote_dma_fused([RemoteDMATransfer(dst_ids=[DstId(rid=rid, pnc=pid)], dma_engine_mask=m["mask"],
+                                                  remote_sem=rsem, srcs=srcs, dsts=[dst_ap], alu_op=1)],
+                               local_sem=S.sent)
+        sent += m["n"]
+
+    if rank is not None:
+        if not lands:
+            g.sync.wait_ge(S.cp, 1)
+            g.sync.dma_start(T.y[:], T.p[:]).then_inc(S.st, 16)
+        else:
+            if mine:
+                g.vector.wait_ge(S.cp, 1)
+            for i, l in enumerate(lands):
+                g.vector.wait_ge(S["arr%d" % l["slot"]], l["n"])
+                if i:
+                    g.vector.wait_ge(S.acc, i)
+                out = T.ysb[:] if i == len(lands) - 1 else T.ps[:]
+                g.vector.tensor_tensor(out, T.ps[:], T["land%d" % l["slot"]][:], AluOpType.add).then_inc(S.acc, 1)
+            g.sync.wait_ge(S.acc, len(lands))
+            g.sync.dma_start(T.y[:], T.ysb[:]).then_inc(S.st, 16)
+        g.sync.wait_ge(S.st, 16)
+    if sent:
+        g.wait_ge(S.sent, sent)

@@ -1,4 +1,3 @@
-from concourse.bass import DstId, RemoteDMATransfer
 from concourse.mybir import AluOpType
 
 F = 256
@@ -17,16 +16,18 @@ SEMAPHORES = ["ld", "mm", "cp", "acc", "st", "sent"] + ["arr%d" % _k for _k in r
 NENG = 8
 
 PLAN = [
-    ("r0", (0,), "h3"), ("r0", (0,), "h1"), ("r0", (0,), "r3"), ("r0", (0,), "r6"), ("r0", (0,), "r1"),
-    ("r1", (1,), "h3"), ("r1", (1,), "h1"), ("r1", (1,), "r3"), ("r1", (1,), "r6"),
-    ("r2", (2,), "h4"), ("r2", (2,), "h2"), ("r2", (2,), "r4"),
-    ("r3", (3,), "h3"), ("r3", (3,), "r6"),
-    ("r4", (4,), "h4"),
+    ("r0", (0,), "A0"), ("r0", (0,), "r1"), ("r0", (0,), "r3"), ("r0", (0,), "r5"),
+    ("r1", (1,), "A1"), ("r1", (1,), "r3"), ("r1", (1,), "r5"), ("r1", (0, 1), "r6"),
+    ("r2", (2,), "A2"), ("r2", (2,), "B2"), ("r2", (2,), "r4"),
+    ("r3", (3,), "A3"), ("r3", (3,), "r5"), ("r3", (3,), "r6"),
+    ("r4", (4,), "A4"),
     ("r5", (5,), "r6"),
-    ("h1", (0, 1), "r2"),
-    ("h2", (2,), "r3"),
-    ("h3", (0, 1, 3), "r4"), ("h3", (0, 1, 3), "r5"),
-    ("h4", (2, 4), "r5"), ("h4", (2, 4), "r6"),
+    ("A0", (0,), "r2"), ("A0", (0,), "r4"),
+    ("A1", (1,), "r4"), ("A1", (1,), "r2"),
+    ("A2", (2,), "r6"), ("A2", (2,), "r5"),
+    ("B2", (2,), "r3"),
+    ("A3", (3,), "r4"),
+    ("A4", (4,), "r5"), ("A4", (4,), "r6"),
 ]
 
 
@@ -48,9 +49,10 @@ def _build(T, topo):
         c = cores[int(name[1:])]
         if name[0] == "r":
             return c
-        return [h for h in range(total)
-                if h not in cores and topo.chip(h) == topo.chip(c) and topo.die(h) == topo.die(c)
-                and all(topo.may_write(h, d) for d in cores)][0]
+        own = [h for h in range(total)
+               if h not in cores and topo.chip(h) == topo.chip(c) and topo.die(h) == topo.die(c)
+               and all(topo.may_write(h, d) for d in cores)]
+        return own["AB".index(name[0])]
 
     msgs = []
     used = {}
@@ -94,28 +96,22 @@ def rank_program(g, core, T, topo):
             g.vector.tensor_copy(T.p[:], T.ps[:]).then_inc(S.cp, 1)
             g.wait_ge(S.cp, 1)
 
-    waited = set()
     sent = 0
+    waited = False
     for m in mine:
-        srcs = []
-        for j in m["terms"]:
-            if j == rank:
-                srcs.append(T.p[:])
-                continue
-            l = [x for x in lands if x["terms"] == (j,)][0]
-            if l["slot"] not in waited:
-                g.wait_ge(S["arr%d" % l["slot"]], l["n"])
-                waited.add(l["slot"])
-            srcs.append(T["land%d" % l["slot"]][:])
-        rid, pid, _se = topo.addr(m["dst"])
-        dst_ap = T["land%d" % m["slot"]][:]
-        rsem = S["arr%d" % m["slot"]]
-        if len(srcs) == 1:
-            g.remote_dma(dst_ap, srcs[0], rsem, S.sent, pid, rid, m["mask"])
+        if rank is None:
+            if not waited:
+                g.wait_ge(S["arr%d" % lands[0]["slot"]], lands[0]["n"])
+                waited = True
+            src = T["land%d" % lands[0]["slot"]][:]
+        elif m["terms"] == (rank,):
+            src = T.p[:]
         else:
-            g.remote_dma_fused([RemoteDMATransfer(dst_ids=[DstId(rid=rid, pnc=pid)], dma_engine_mask=m["mask"],
-                                                  remote_sem=rsem, srcs=srcs, dsts=[dst_ap], alu_op=1)],
-                               local_sem=S.sent)
+            assert m["terms"] == tuple(range(rank + 1))
+            g.wait_ge(S.acc, len(lands))
+            src = T.ysb[:]
+        rid, pid, _se = topo.addr(m["dst"])
+        g.remote_dma(T["land%d" % m["slot"]][:], src, S["arr%d" % m["slot"]], S.sent, pid, rid, m["mask"])
         sent += m["n"]
 
     if rank is not None:

from concourse.mybir import AluOpType

F = 256
NLAND = 5
SCRATCH = {
    "a_sb": ("sbuf", [128, 128], "bfloat16"),
    "w_sb": ("sbuf", [128, F], "bfloat16"),
    "ps": ("psum", [128, F], "float32"),
    "p": ("sbuf", [128, F], "bfloat16"),
    "ysb": ("sbuf", [128, F], "bfloat16"),
}
for _k in range(NLAND):
    SCRATCH["land%d" % _k] = ("sbuf", [128, F], "bfloat16")
SEMAPHORES = ["ld", "mm", "cp", "acc", "st", "sent"] + ["arr%d" % _k for _k in range(NLAND)]

NENG = 8

PLAN = [
    ("r0", (0,), "A0"), ("r0", (0,), "r1"), ("r0", (0,), "r3"), ("r0", (0,), "r5"),
    ("r1", (1,), "A1"), ("r1", (1,), "r3"), ("r1", (1,), "r5"), ("r1", (0, 1), "r6"),
    ("r2", (2,), "A2"), ("r2", (2,), "B2"), ("r2", (2,), "r4"),
    ("r3", (3,), "A3"), ("r3", (3,), "r5"), ("r3", (3,), "r6"),
    ("r4", (4,), "A4"),
    ("r5", (5,), "r6"),
    ("A0", (0,), "r2"), ("A0", (0,), "r4"),
    ("A1", (1,), "r4"), ("A1", (1,), "r2"),
    ("A2", (2,), "r6"), ("A2", (2,), "r5"),
    ("B2", (2,), "r3"),
    ("A3", (3,), "r4"),
    ("A4", (4,), "r5"), ("A4", (4,), "r6"),
]


def _bits(mask, n):
    out, got, e = 0, 0, 0
    while got < n:
        if (mask >> e) & 1:
            out |= 1 << e
            got += 1
        e += 1
    return out


def _build(T, topo):
    cores = list(T.cores)
    total = topo.CORES_PER_CHIP * topo.CHIPS

    def node(name):
        c = cores[int(name[1:])]
        if name[0] == "r":
            return c
        own = [h for h in range(total)
               if h not in cores and topo.chip(h) == topo.chip(c) and topo.die(h) == topo.die(c)
               and all(topo.may_write(h, d) for d in cores)]
        return own["AB".index(name[0])]

    msgs = []
    used = {}
    pos = {}
    for s, terms, d in PLAN:
        src, dst = node(s), node(d)
        assert topo.may_write(src, dst)
        slot = used.get(dst, 0)
        used[dst] = slot + 1
        pos[src] = pos.get(src, 0) + 1
        msgs.append({"src": src, "dst": dst, "terms": terms, "slot": slot,
                     "when": (0 if s[0] == "r" else 1, pos[src])})
    for m in msgs:
        common = -1
        for o in msgs:
            if o["src"] == m["src"]:
                common &= topo.mask(o["src"], o["dst"])
        m["mask"] = _bits(common, NENG)
        m["n"] = NENG
    return msgs


def rank_program(g, core, T, topo):
    msgs = _build(T, topo)
    rank = T.rank_of(core)
    mine = [m for m in msgs if m["src"] == core]
    lands = sorted([m for m in msgs if m["dst"] == core], key=lambda m: m["when"])
    if rank is None and not mine:
        return
    S = T.sem

    if rank is not None:
        got = sorted([rank] + [j for m in lands for j in m["terms"]])
        assert got == list(range(rank + 1))
        g.sync.dma_start(T.a_sb[:], T.a[:]).then_inc(S.ld, 16)
        g.scalar.dma_start(T.w_sb[:], T.w[:]).then_inc(S.ld, 16)
        g.tensor.wait_ge(S.ld, 32)
        g.tensor.matmul(T.ps[:], T.a_sb[:], T.w_sb[:], True, True).then_inc(S.mm, 1)
        g.vector.wait_ge(S.mm, 1)
        if mine or not lands:
            g.vector.tensor_copy(T.p[:], T.ps[:]).then_inc(S.cp, 1)
            g.wait_ge(S.cp, 1)

    sent = 0
    waited = False
    for m in mine:
        if rank is None:
            if not waited:
                g.wait_ge(S["arr%d" % lands[0]["slot"]], lands[0]["n"])
                waited = True
            src = T["land%d" % lands[0]["slot"]][:]
        elif m["terms"] == (rank,):
            src = T.p[:]
        else:
            assert m["terms"] == tuple(range(rank + 1))
            g.wait_ge(S.acc, len(lands))
            src = T.ysb[:]
        rid, pid, _se = topo.addr(m["dst"])
        g.remote_dma(T["land%d" % m["slot"]][:], src, S["arr%d" % m["slot"]], S.sent, pid, rid, m["mask"])
        sent += m["n"]

    if rank is not None:
        if not lands:
            g.sync.wait_ge(S.cp, 1)
            g.sync.dma_start(T.y[:], T.p[:]).then_inc(S.st, 16)
        else:
            if mine:
                g.vector.wait_ge(S.cp, 1)
            for i, l in enumerate(lands):
                g.vector.wait_ge(S["arr%d" % l["slot"]], l["n"])
                if i:
                    g.vector.wait_ge(S.acc, i)
                out = T.ysb[:] if i == len(lands) - 1 else T.ps[:]
                g.vector.tensor_tensor(out, T.ps[:], T["land%d" % l["slot"]][:], AluOpType.add).then_inc(S.acc, 1)
            g.sync.wait_ge(S.acc, len(lands))
            g.sync.dma_start(T.y[:], T.ysb[:]).then_inc(S.st, 16)
        g.sync.wait_ge(S.st, 16)
    if sent:
        g.wait_ge(S.sent, sent)
